import numpy as np, ml_dtypes
CORES = [113,118,241,246]
N = 4
import mx_ref
NC, G = 128, 2
C = np.float32(0.023)
BF = ml_dtypes.bfloat16
def cut(t, i, w=512):
    return t[:, w * i:w * i + w]
def tile(rs):
    return np.stack(rs, axis=2).reshape(128, -1).astype(BF)
def layer(w, X):
    out = []
    for i in range(G):
        for t in range(len(X)):
            p = mx_ref.matmul(mx_ref.quantize(cut(w, len(X) * i + t)), X[t])
            z = p if t == 0 else z + p
        out.append(z)
    return out
def act(Z):
    return [np.maximum(s * z, 0) * C for z in Z for s in (1, -1)]
def pick(b):
    s = np.zeros((128, 128, 4), np.float32)
    s[np.arange(128), np.arange(128), b] = 1.0
    return mx_ref.quantize(s.reshape(128, 512).astype(BF))
def setup_inputs(rng):
    def f(*shape):
        return mx_ref.flush((rng.standard_normal(shape, dtype=np.float32) * np.exp2(rng.integers(-2, 3, shape[:-1] + (1,)))).astype(BF))
    return {"x": f(N, 128, 4 * NC), "w1": f(N, 128, G * 512), "w2": f(N, 128, 512), "a": f(N, 128, G * 512), "b": f(N, 128, N * 4 * NC)}
def setup_inputs_blocks(rng):
    d = setup_inputs(rng)
    for k in ("x", "w1", "w2", "a", "b"): d[k] = mx_ref.spread(d[k], rng, 2)
    return d
def setup_inputs_wide(rng):
    d = setup_inputs(rng)
    for k in ("x", "w1", "w2", "a", "b"): d[k] = mx_ref.flush((d[k].astype(np.float32) * np.exp2(rng.integers(-6, 7, (N, 1, 1))).astype(np.float32)).astype(BF))
    return d
def setup_inputs_zeros(rng):
    d = setup_inputs(rng); v = d["x"].reshape(N, 128, -1, 4).copy()
    v[np.broadcast_to((rng.random((N, 1, v.shape[2], 1)) < 0.33), v.shape)] = 0
    d["x"] = v.reshape(d["x"].shape)
    return d
def reference(x, w1, w2, a, b):
    H = [mx_ref.quantize(tile(act(layer(w1[j], [mx_ref.quantize(x[j])])))) for j in range(N)]
    y = np.zeros((N, 128, N * NC), np.float32)
    for r in range(N):
        qw = mx_ref.quantize(w2[r])
        for j in range(N):
            y[r][:, NC * j:NC * j + NC] = mx_ref.matmul(qw, H[j])
    S = [pick(t) for t in range(4)]
    z = np.zeros((N, 128, NC, 4), np.float32)
    for c in range(N):
        for r in range(N):
            q = mx_ref.quantize(tile(act(layer(a[r], [mx_ref.quantize(cut(b[r], c, 4 * NC))]))))
            p = np.stack([mx_ref.matmul(S[t], q) for t in range(4)], axis=2)
            z[c] = p if r == 0 else z[c] + p
    return {"y": y, "z": z.reshape(N, 128, 4 * NC)}

@@ -1,0 +1,256 @@
+import numpy as np
+from concourse.bass import DstId, RemoteDMATransfer
+from concourse.mybir import dt, AluOpType, ActivationFunctionType as AF
+
+NC = 128
+W = 4 * NC
+C = float(np.float32(0.023))
+
+SCRATCH = {
+    "xt": ("sbuf", [128, W], "bfloat16"),
+    "w1t": ("sbuf", [128, 2 * W], "bfloat16"),
+    "w2t": ("sbuf", [128, W], "bfloat16"),
+    "at": ("sbuf", [128, 2 * W], "bfloat16"),
+    "bt": ("sbuf", [128, 4 * W], "bfloat16"),
+    "et": ("sbuf", [128, W + 4], "bfloat16"),
+    "ht": ("sbuf", [128, W], "bfloat16"),
+    "got": ("sbuf", [128, 2 * W], "bfloat16"),
+    "gnt": ("sbuf", [128, 2 * W], "bfloat16"),
+    "xq": ("sbuf", [128, NC], "float8_e4m3fn_x4"), "xs": ("sbuf", [128, NC], "uint8"),
+    "w1q": ("sbuf", [128, 2 * NC], "float8_e4m3fn_x4"), "w1s": ("sbuf", [128, 2 * NC], "uint8"),
+    "w2q": ("sbuf", [128, NC], "float8_e4m3fn_x4"), "w2s": ("sbuf", [128, NC], "uint8"),
+    "aq": ("sbuf", [128, 2 * NC], "float8_e4m3fn_x4"), "as_": ("sbuf", [128, 2 * NC], "uint8"),
+    "bq": ("sbuf", [128, 4 * NC], "float8_e4m3fn_x4"), "bs": ("sbuf", [128, 4 * NC], "uint8"),
+    "sq": ("sbuf", [128, 4 * NC], "float8_e4m3fn_x4"), "ss": ("sbuf", [128, 4 * NC], "uint8"),
+    "goq": ("sbuf", [128, 2 * NC], "float8_e4m3fn_x4"), "gos": ("sbuf", [128, 2 * NC], "uint8"),
+    "nq": ("sbuf", [128, 4 * NC], "float8_e4m3fn_x4"), "ns": ("sbuf", [128, 4 * NC], "uint8"),
+    "hlq": ("sbuf", [128, 2 * NC], "float8_e4m3fn_x4"), "hls": ("sbuf", [128, 2 * NC], "uint8"),
+    "glq": ("sbuf", [128, 2 * NC], "float8_e4m3fn_x4"), "gls": ("sbuf", [128, 2 * NC], "uint8"),
+    "plq": ("sbuf", [128, 2 * NC], "float8_e4m3fn_x4"), "pls": ("sbuf", [128, 2 * NC], "uint8"),
+    "yt": ("sbuf", [128, 4 * NC], "float32"),
+    "zt": ("sbuf", [128, W], "float32"),
+    "p0": ("psum", [128, 512], "float32"), "p1": ("psum", [128, 512], "float32"),
+    "p2": ("psum", [128, 512], "float32"), "p3": ("psum", [128, 512], "float32"),
+    "p4": ("psum", [128, 512], "float32"), "p5": ("psum", [128, 512], "float32"),
+    "p6": ("psum", [128, 512], "float32"), "p7": ("psum", [128, 512], "float32"),
+}
+SEMAPHORES = [
+    "ldx", "ldw1", "lda", "ldb1", "ldb2", "ldbn", "ldw2",
+    "e0", "e1", "qs", "qx0", "qw", "qa0", "qa1", "qb2", "qbn", "qw2",
+    "zh0", "zh1", "z10", "z11", "z20", "z21", "zn0", "zn1",
+    "ah", "a1", "a2", "an", "hq", "g1q", "g2q", "gnq",
+    "yo", "yp", "yf", "ycn", "ycf", "d0", "d1", "d2", "d3", "za", "zb",
+    "hin", "g1in", "g2in", "pin", "sent", "sty", "stz", "stb",
+]
+
+
+def rank_program(g, core, T, topo):
+    r = T.rank_of(core)
+    if r is None:
+        return
+    cores = T.cores
+    n = len(cores)
+    S = T.sem
+
+    def near_of(k):
+        return [c for c in range(n) if topo.host(cores[c]) == topo.host(cores[k]) and topo.chip(cores[c]) == topo.chip(cores[k])]
+
+    def far_of(k):
+        nk = near_of(k)
+        return [c for c in range(n) if c not in nk]
+
+    def same_die(j, k):
+        return topo.die(cores[j]) == topo.die(cores[k])
+
+    near, far = near_of(r), far_of(r)
+    p = [c for c in near if c != r][0]
+    f1 = [c for c in far if same_die(c, r)][0]
+    f2 = [c for c in far if c != f1][0]
+    own_i, p_i = near.index(r), near.index(p)
+
+    def col(i, w=NC, k=1):
+        return slice(i * w, (i + k) * w)
+
+    def dst(c):
+        rid, pid = topo.addr(cores[c], core)
+        return DstId(rid=rid, pnc=pid)
+
+    def quant(q, s, qi, src, lo, k=1):
+        return g.vector.quantize_mx(q[:, col(qi, NC, k)], s[:, col(qi, NC, k)], src[:, lo:lo + k * W])
+
+    def mm(bank, lq, ls, li, rq, rs, ri, k=1, start=True, stop=True):
+        return g.tensor.matmul_mx(bank[:, 0:k * NC], lq[:, col(li)], ls[:, col(li)],
+                                  rq[:, col(ri, NC, k)], rs[:, col(ri, NC, k)], start, stop)
+
+    def act_s(tile, lo, b, bank, k=1):
+        return g.scalar.activation(tile[:, lo + b:lo + k * W:4], bank[:, 0:k * NC], AF.Relu, scale=C if b % 2 == 0 else -C)
+
+    def act_v(tile, lo, b, bank, k=1):
+        return g.vector.tensor_scalar(tile[:, lo + b:lo + k * W:4], bank[:, 0:k * NC], C if b % 2 == 0 else -C, 0.0,
+                                      AluOpType.mult, AluOpType.max)
+
+    h_i = 0 if p_i == 0 else 3
+    pv = col(0, NC, 2) if p_i == 0 else col(2, NC, 2)
+    pp_i = near_of(p).index(r)
+    ph_i, pg_i = (0, 1) if pp_i == 0 else (1, 0)
+
+    g.sync.dma_start(T.xt[:], T.x[:, :]).then_inc(S.ldx, 16)
+    g.scalar.dma_start(T.w1t[:], T.w1[:, :]).then_inc(S.ldw1, 16)
+    g.sync.dma_start(T.at[:], T.a[:, :]).then_inc(S.lda, 16)
+    g.scalar.dma_start(T.bt[:, col(f1, W)], T.b[:, col(f1, W)]).then_inc(S.ldb1, 16)
+    g.sync.dma_start(T.bt[:, col(f2, W)], T.b[:, col(f2, W)]).then_inc(S.ldb2, 16)
+    g.scalar.dma_start(T.bt[:, col(near[0], W, 2)], T.b[:, col(near[0], W, 2)]).then_inc(S.ldbn, 16)
+    g.sync.dma_start(T.w2t[:], T.w2[:, :]).then_inc(S.ldw2, 16)
+
+    v = g.vector
+    v.memset(T.et[:], 0.0).then_inc(S.e0, 1)
+    v.wait_ge(S.e1, 1)
+    for b in range(4):
+        quant(T.sq, T.ss, b, T.et, 3 - b).then_inc(S.qs, 1)
+    v.wait_ge(S.ldx, 16)
+    quant(T.xq, T.xs, 0, T.xt, 0).then_inc(S.qx0, 1)
+    v.wait_ge(S.ldw1, 16)
+    quant(T.w1q, T.w1s, 0, T.w1t, 0).then_inc(S.qx0, 1)
+    quant(T.w1q, T.w1s, 1, T.w1t, W).then_inc(S.qw, 1)
+    v.wait_ge(S.zh1, 1)
+    act_v(T.ht, 0, 2, T.p1).then_inc(S.ah, 1)
+    act_v(T.ht, 0, 3, T.p1).then_inc(S.ah, 1)
+    v.wait_ge(S.ah, 4)
+    quant(T.nq, T.ns, h_i, T.ht, 0).then_inc(S.hq, 1)
+    v.wait_ge(S.lda, 16)
+    quant(T.aq, T.as_, 0, T.at, 0).then_inc(S.qa0, 1)
+    v.wait_ge(S.ldb1, 16)
+    quant(T.bq, T.bs, f1, T.bt, f1 * W).then_inc(S.qa0, 1)
+    quant(T.aq, T.as_, 1, T.at, W).then_inc(S.qa1, 1)
+    v.wait_ge(S.ldb2, 16)
+    quant(T.bq, T.bs, f2, T.bt, f2 * W).then_inc(S.qb2, 1)
+    v.wait_ge(S.z11, 1)
+    act_v(T.got, 0, 2, T.p3).then_inc(S.a1, 1)
+    act_v(T.got, 0, 3, T.p3).then_inc(S.a1, 1)
+    v.wait_ge(S.a1, 4)
+    quant(T.goq, T.gos, 0, T.got, 0).then_inc(S.g1q, 1)
+    v.wait_ge(S.z21, 1)
+    act_v(T.got, W, 2, T.p5).then_inc(S.a2, 1)
+    act_v(T.got, W, 3, T.p5).then_inc(S.a2, 1)
+    v.wait_ge(S.a2, 4)
+    quant(T.goq, T.gos, 1, T.got, W).then_inc(S.g2q, 1)
+    v.wait_ge(S.ldbn, 16)
+    quant(T.bq, T.bs, near[0], T.bt, near[0] * W, 2).then_inc(S.qbn, 1)
+    v.wait_ge(S.ldw2, 16)
+    quant(T.w2q, T.w2s, 0, T.w2t, 0).then_inc(S.qw2, 1)
+    v.wait_ge(S.zn1, 1)
+    act_v(T.gnt, 0, 2, T.p7, 2).then_inc(S.an, 1)
+    act_v(T.gnt, 0, 3, T.p7, 2).then_inc(S.an, 1)
+    v.wait_ge(S.an, 4)
+    quant(T.nq, T.ns, 1, T.gnt, 0, 2).then_inc(S.gnq, 1)
+    v.wait_ge(S.yf, 1)
+    v.tensor_copy(T.yt[:, col(far[0], NC, 2)], T.p1[:, 0:2 * NC]).then_inc(S.ycf, 1)
+    hw, hn = W // 2, NC // 2
+    v.wait_ge(S.d0, 1)
+    v.tensor_copy(T.zt[:, 0:hw:4], T.p2[:, 0:hn]).then_inc(S.za, 1)
+    v.wait_ge(S.d1, 1)
+    v.tensor_copy(T.zt[:, 1:hw:4], T.p3[:, 0:hn]).then_inc(S.za, 1)
+    v.tensor_copy(T.zt[:, hw:W:4], T.p2[:, hn:NC]).then_inc(S.zb, 1)
+    v.tensor_copy(T.zt[:, hw + 1:W:4], T.p3[:, hn:NC]).then_inc(S.zb, 1)
+
+    t = g.tensor
+    t.wait_ge(S.qx0, 2)
+    mm(T.p0, T.w1q, T.w1s, 0, T.xq, T.xs, 0).then_inc(S.zh0, 1)
+    t.wait_ge(S.qw, 1)
+    mm(T.p1, T.w1q, T.w1s, 1, T.xq, T.xs, 0).then_inc(S.zh1, 1)
+    t.wait_ge(S.qa0, 2)
+    mm(T.p2, T.aq, T.as_, 0, T.bq, T.bs, f1).then_inc(S.z10, 1)
+    t.wait_ge(S.qa1, 1)
+    mm(T.p3, T.aq, T.as_, 1, T.bq, T.bs, f1).then_inc(S.z11, 1)
+    t.wait_ge(S.qb2, 1)
+    mm(T.p4, T.aq, T.as_, 0, T.bq, T.bs, f2).then_inc(S.z20, 1)
+    mm(T.p5, T.aq, T.as_, 1, T.bq, T.bs, f2).then_inc(S.z21, 1)
+    t.wait_ge(S.qbn, 1)
+    mm(T.p6, T.aq, T.as_, 0, T.bq, T.bs, near[0], 2).then_inc(S.zn0, 1)
+    mm(T.p7, T.aq, T.as_, 1, T.bq, T.bs, near[0], 2).then_inc(S.zn1, 1)
+    t.wait_ge(S.hq, 1)
+    t.wait_ge(S.qw2, 1)
+    mm(T.p0, T.w2q, T.w2s, 0, T.nq, T.ns, h_i).then_inc(S.yo, 1)
+    t.wait_ge(S.qs, 4)
+    t.wait_ge(S.g1q, 1)
+    t.wait_ge(S.g2q, 1)
+    t.wait_ge(S.gnq, 1)
+    banks = [T.p2, T.p3, T.p4, T.p5]
+    order = [0, 2, 1, 3]
+    for b in order:
+        mm(banks[b], T.sq, T.ss, b, T.nq, T.ns, 1 + own_i, 1, True, False)
+    t.wait_ge(S.hin, 32)
+    mm(T.p1, T.w2q, T.w2s, 0, T.hlq, T.hls, 0, 2).then_inc(S.yf, 1)
+    t.wait_ge(S.pin, 16)
+    mm(T.p6, T.w2q, T.w2s, 0, T.plq, T.pls, ph_i).then_inc(S.yp, 1)
+    for b in order:
+        mm(banks[b], T.sq, T.ss, b, T.plq, T.pls, pg_i, 1, False, False)
+    t.wait_ge(S.g1in, 16)
+    for b in order:
+        mm(banks[b], T.sq, T.ss, b, T.glq, T.gls, 0, 1, False, False)
+    t.wait_ge(S.g2in, 16)
+    for b in order:
+        mm(banks[b], T.sq, T.ss, b, T.glq, T.gls, 1, 1, False, True).then_inc(S["d%d" % b], 1)
+
+    s = g.scalar
+    s.wait_ge(S.zh0, 1)
+    act_s(T.ht, 0, 0, T.p0).then_inc(S.ah, 1)
+    act_s(T.ht, 0, 1, T.p0).then_inc(S.ah, 1)
+    s.wait_ge(S.z10, 1)
+    act_s(T.got, 0, 0, T.p2).then_inc(S.a1, 1)
+    act_s(T.got, 0, 1, T.p2).then_inc(S.a1, 1)
+    s.wait_ge(S.z20, 1)
+    act_s(T.got, W, 0, T.p4).then_inc(S.a2, 1)
+    act_s(T.got, W, 1, T.p4).then_inc(S.a2, 1)
+    s.wait_ge(S.zn0, 1)
+    act_s(T.gnt, 0, 0, T.p6, 2).then_inc(S.an, 1)
+    act_s(T.gnt, 0, 1, T.p6, 2).then_inc(S.an, 1)
+    s.wait_ge(S.yo, 1)
+    s.activation(T.yt[:, col(r)], T.p0[:, 0:NC], AF.Copy).then_inc(S.ycn, 1)
+    s.wait_ge(S.yp, 1)
+    s.activation(T.yt[:, col(p)], T.p6[:, 0:NC], AF.Copy).then_inc(S.ycn, 1)
+    s.wait_ge(S.d2, 1)
+    s.activation(T.zt[:, 2:hw:4], T.p4[:, 0:hn], AF.Copy).then_inc(S.za, 1)
+    s.wait_ge(S.d3, 1)
+    s.activation(T.zt[:, 3:hw:4], T.p5[:, 0:hn], AF.Copy).then_inc(S.za, 1)
+    s.activation(T.zt[:, hw + 2:W:4], T.p4[:, hn:NC], AF.Copy).then_inc(S.zb, 1)
+    s.activation(T.zt[:, hw + 3:W:4], T.p5[:, hn:NC], AF.Copy).then_inc(S.zb, 1)
+    s.wait_ge(S.zb, 4)
+    s.dma_start(T.z[:, hw:W], T.zt[:, hw:W]).then_inc(S.stb, 16)
+    s.wait_ge(S.stb, 16)
+
+    g.sync.wait_ge(S.ycf, 1)
+    g.sync.dma_start(T.y[:, col(far[0], NC, 2)], T.yt[:, col(far[0], NC, 2)]).then_inc(S.sty, 16)
+    g.sync.wait_ge(S.ycn, 2)
+    g.sync.dma_start(T.y[:, col(near[0], NC, 2)], T.yt[:, col(near[0], NC, 2)]).then_inc(S.sty, 16)
+    g.sync.wait_ge(S.za, 4)
+    g.sync.dma_start(T.z[:, 0:hw], T.zt[:, 0:hw]).then_inc(S.stz, 16)
+    g.sync.wait_ge(S.sty, 32)
+    g.sync.wait_ge(S.stz, 16)
+
+    g.wait_ge(S.e0, 1)
+    ev = T.et[:, 3:W + 3:4]
+    g.affine_select(ev, ev, [[-1, NC]], AluOpType.not_equal, 1.0, 0, 1).then_inc(S.e1, 1)
+
+    off_mask = topo.mask(core, cores[f1])
+    on_mask = topo.mask(core, cores[p]) & ~off_mask
+    slot = {c: far_of(c).index(r) for c in far}
+    g.wait_ge(S.hq, 1)
+    g.remote_dma_fused([RemoteDMATransfer(
+        dst_ids=[dst(c) for c in (f1, f2)], dma_engine_mask=off_mask, remote_sem=S.hin,
+        srcs=[T.nq[:, col(h_i)].bitcast(dt.uint8)],
+        dsts=[T.hlq[:, col(slot[c])].bitcast(dt.uint8) for c in (f1, f2)])], local_sem=S.sent)
+    g.remote_dma_fused([RemoteDMATransfer(
+        dst_ids=[dst(c) for c in (f1, f2)], dma_engine_mask=off_mask, remote_sem=S.hin,
+        srcs=[T.ns[:, col(h_i)]], dsts=[T.hls[:, col(slot[c])] for c in (f1, f2)])], local_sem=S.sent)
+    for i, c in enumerate((f1, f2)):
+        rid, pid = topo.addr(cores[c], core)
+        sem = S["g%din" % (i + 1)]
+        g.wait_ge(S["g%dq" % (i + 1)], 1)
+        g.remote_dma(T.glq[:, col(i)].bitcast(dt.uint8), T.goq[:, col(i)].bitcast(dt.uint8), sem, S.sent, pid, rid, off_mask)
+        g.remote_dma(T.gls[:, col(i)], T.gos[:, col(i)], sem, S.sent, pid, rid, off_mask)
+    rid, pid = topo.addr(cores[p], core)
+    g.wait_ge(S.gnq, 1)
+    g.remote_dma(T.plq[:].bitcast(dt.uint8), T.nq[:, pv].bitcast(dt.uint8), S.pin, S.sent, pid, rid, on_mask)
+    g.remote_dma(T.pls[:], T.ns[:, pv], S.pin, S.sent, pid, rid, on_mask)
+    g.wait_ge(S.sent, 8 * off_mask.bit_count())

@@ -5,6 +5,9 @@ from concourse.mybir import dt, AluOpType, ActivationFunctionType as AF
 NC = 128
 W = 4 * NC
 C = float(np.float32(0.023))
+JOBS = ["f2", "f1", "h", "p", "o"]
+SLOT = {j: i for i, j in enumerate(JOBS)}
+LAND = {"f2": 0, "f1": 1, "p": 2, "hp": 3, "h1": 4, "h2": 5}
 
 SCRATCH = {
     "xt": ("sbuf", [128, W], "bfloat16"),
@@ -13,35 +16,25 @@ SCRATCH = {
     "at": ("sbuf", [128, 2 * W], "bfloat16"),
     "bt": ("sbuf", [128, 4 * W], "bfloat16"),
     "et": ("sbuf", [128, W + 4], "bfloat16"),
-    "ht": ("sbuf", [128, W], "bfloat16"),
-    "got": ("sbuf", [128, 2 * W], "bfloat16"),
-    "gnt": ("sbuf", [128, 2 * W], "bfloat16"),
+    "tl": ("sbuf", [128, 5 * W], "bfloat16"),
     "xq": ("sbuf", [128, NC], "float8_e4m3fn_x4"), "xs": ("sbuf", [128, NC], "uint8"),
     "w1q": ("sbuf", [128, 2 * NC], "float8_e4m3fn_x4"), "w1s": ("sbuf", [128, 2 * NC], "uint8"),
     "w2q": ("sbuf", [128, NC], "float8_e4m3fn_x4"), "w2s": ("sbuf", [128, NC], "uint8"),
     "aq": ("sbuf", [128, 2 * NC], "float8_e4m3fn_x4"), "as_": ("sbuf", [128, 2 * NC], "uint8"),
     "bq": ("sbuf", [128, 4 * NC], "float8_e4m3fn_x4"), "bs": ("sbuf", [128, 4 * NC], "uint8"),
     "sq": ("sbuf", [128, 4 * NC], "float8_e4m3fn_x4"), "ss": ("sbuf", [128, 4 * NC], "uint8"),
-    "goq": ("sbuf", [128, 2 * NC], "float8_e4m3fn_x4"), "gos": ("sbuf", [128, 2 * NC], "uint8"),
-    "nq": ("sbuf", [128, 4 * NC], "float8_e4m3fn_x4"), "ns": ("sbuf", [128, 4 * NC], "uint8"),
-    "hlq": ("sbuf", [128, 2 * NC], "float8_e4m3fn_x4"), "hls": ("sbuf", [128, 2 * NC], "uint8"),
-    "glq": ("sbuf", [128, 2 * NC], "float8_e4m3fn_x4"), "gls": ("sbuf", [128, 2 * NC], "uint8"),
-    "plq": ("sbuf", [128, 2 * NC], "float8_e4m3fn_x4"), "pls": ("sbuf", [128, 2 * NC], "uint8"),
+    "mq": ("sbuf", [128, 5 * NC], "float8_e4m3fn_x4"), "ms": ("sbuf", [128, 5 * NC], "uint8"),
+    "lq": ("sbuf", [128, 6 * NC], "float8_e4m3fn_x4"), "ls": ("sbuf", [128, 6 * NC], "uint8"),
     "yt": ("sbuf", [128, 4 * NC], "float32"),
     "zt": ("sbuf", [128, W], "float32"),
-    "p0": ("psum", [128, 512], "float32"), "p1": ("psum", [128, 512], "float32"),
-    "p2": ("psum", [128, 512], "float32"), "p3": ("psum", [128, 512], "float32"),
-    "p4": ("psum", [128, 512], "float32"), "p5": ("psum", [128, 512], "float32"),
-    "p6": ("psum", [128, 512], "float32"), "p7": ("psum", [128, 512], "float32"),
 }
-SEMAPHORES = [
-    "ldx", "ldw1", "lda", "ldb1", "ldb2", "ldbn", "ldw2",
-    "e0", "e1", "qs", "qx0", "qw", "qa0", "qa1", "qb2", "qbn", "qw2",
-    "zh0", "zh1", "z10", "z11", "z20", "z21", "zn0", "zn1",
-    "ah", "a1", "a2", "an", "hq", "g1q", "g2q", "gnq",
-    "yo", "yp", "yf", "ycn", "ycf", "d0", "d1", "d2", "d3", "za", "zb",
-    "hin", "g1in", "g2in", "pin", "sent", "sty", "stz", "stb",
-]
+for k in range(8):
+    SCRATCH["p%d" % k] = ("psum", [128, 512], "float32")
+SEMAPHORES = ["ldx", "ldw1", "lda", "ldw2", "e0", "e1", "qs", "qx", "qw0", "qw1", "qa0", "qa1", "qw2",
+              "yo", "yp", "y1", "y2", "yc1", "yc2", "ycn", "d0", "d1", "d2", "d3", "za",
+              "h1in", "h2in", "hpin", "f1in", "f2in", "pin", "sent", "styn", "sty1", "sty2", "stz"]
+for j in JOBS:
+    SEMAPHORES += ["ld" + j, "q" + j, "z0" + j, "z1" + j, "v1" + j, "ac" + j, "mq" + j]
 
 
 def rank_program(g, core, T, topo):
@@ -52,21 +45,15 @@ def rank_program(g, core, T, topo):
     n = len(cores)
     S = T.sem
 
-    def near_of(k):
-        return [c for c in range(n) if topo.host(cores[c]) == topo.host(cores[k]) and topo.chip(cores[c]) == topo.chip(cores[k])]
-
-    def far_of(k):
-        nk = near_of(k)
-        return [c for c in range(n) if c not in nk]
-
-    def same_die(j, k):
-        return topo.die(cores[j]) == topo.die(cores[k])
-
-    near, far = near_of(r), far_of(r)
+    near = [c for c in range(n) if topo.host(cores[c]) == topo.host(core) and topo.chip(cores[c]) == topo.chip(core)]
+    far = [c for c in range(n) if c not in near]
     p = [c for c in near if c != r][0]
-    f1 = [c for c in far if same_die(c, r)][0]
+    f1 = [c for c in far if topo.die(cores[c]) == topo.die(core)][0]
     f2 = [c for c in far if c != f1][0]
-    own_i, p_i = near.index(r), near.index(p)
+    rank = {"f1": f1, "f2": f2, "p": p, "o": r}
+    P = [T["p%d" % k] for k in range(8)]
+    bank = {j: (P[2 * i % 8], P[2 * i % 8 + 1]) for i, j in enumerate(JOBS)}
+    zb = P[2:6]
 
     def col(i, w=NC, k=1):
         return slice(i * w, (i + k) * w)
@@ -75,158 +62,138 @@ def rank_program(g, core, T, topo):
         rid, pid = topo.addr(cores[c], core)
         return DstId(rid=rid, pnc=pid)
 
-    def quant(q, s, qi, src, lo, k=1):
-        return g.vector.quantize_mx(q[:, col(qi, NC, k)], s[:, col(qi, NC, k)], src[:, lo:lo + k * W])
+    def quant(q, s, qi, src, lo):
+        return g.vector.quantize_mx(q[:, col(qi)], s[:, col(qi)], src[:, lo:lo + W])
 
-    def mm(bank, lq, ls, li, rq, rs, ri, k=1, start=True, stop=True):
-        return g.tensor.matmul_mx(bank[:, 0:k * NC], lq[:, col(li)], ls[:, col(li)],
-                                  rq[:, col(ri, NC, k)], rs[:, col(ri, NC, k)], start, stop)
+    def mm(out, lq, ls, li, rq, rs, ri, start=True, stop=True):
+        return g.tensor.matmul_mx(out[:, 0:NC], lq[:, col(li)], ls[:, col(li)], rq[:, col(ri)], rs[:, col(ri)], start, stop)
 
-    def act_s(tile, lo, b, bank, k=1):
-        return g.scalar.activation(tile[:, lo + b:lo + k * W:4], bank[:, 0:k * NC], AF.Relu, scale=C if b % 2 == 0 else -C)
+    def result(j, b):
+        lo = SLOT[j] * W
+        return T.tl[:, lo + b:lo + W:4], bank[j][b // 2][:, 0:NC], C if b % 2 == 0 else -C
 
-    def act_v(tile, lo, b, bank, k=1):
-        return g.vector.tensor_scalar(tile[:, lo + b:lo + k * W:4], bank[:, 0:k * NC], C if b % 2 == 0 else -C, 0.0,
-                                      AluOpType.mult, AluOpType.max)
+    def load_b(q, j):
+        c = col(rank[j], W)
+        q.dma_start(T.bt[:, c], T.b[:, c]).then_inc(S["ld" + j], 16)
 
-    h_i = 0 if p_i == 0 else 3
-    pv = col(0, NC, 2) if p_i == 0 else col(2, NC, 2)
-    pp_i = near_of(p).index(r)
-    ph_i, pg_i = (0, 1) if pp_i == 0 else (1, 0)
-
-    g.sync.dma_start(T.xt[:], T.x[:, :]).then_inc(S.ldx, 16)
-    g.scalar.dma_start(T.w1t[:], T.w1[:, :]).then_inc(S.ldw1, 16)
     g.sync.dma_start(T.at[:], T.a[:, :]).then_inc(S.lda, 16)
-    g.scalar.dma_start(T.bt[:, col(f1, W)], T.b[:, col(f1, W)]).then_inc(S.ldb1, 16)
-    g.sync.dma_start(T.bt[:, col(f2, W)], T.b[:, col(f2, W)]).then_inc(S.ldb2, 16)
-    g.scalar.dma_start(T.bt[:, col(near[0], W, 2)], T.b[:, col(near[0], W, 2)]).then_inc(S.ldbn, 16)
+    load_b(g.scalar, "f2")
+    g.sync.dma_start(T.xt[:], T.x[:, :]).then_inc(S.ldx, 16)
+    load_b(g.scalar, "f1")
+    load_b(g.sync, "p")
+    g.scalar.dma_start(T.w1t[:], T.w1[:, :]).then_inc(S.ldw1, 16)
     g.sync.dma_start(T.w2t[:], T.w2[:, :]).then_inc(S.ldw2, 16)
+    load_b(g.scalar, "o")
 
     v = g.vector
     v.memset(T.et[:], 0.0).then_inc(S.e0, 1)
     v.wait_ge(S.e1, 1)
     for b in range(4):
         quant(T.sq, T.ss, b, T.et, 3 - b).then_inc(S.qs, 1)
-    v.wait_ge(S.ldx, 16)
-    quant(T.xq, T.xs, 0, T.xt, 0).then_inc(S.qx0, 1)
-    v.wait_ge(S.ldw1, 16)
-    quant(T.w1q, T.w1s, 0, T.w1t, 0).then_inc(S.qx0, 1)
-    quant(T.w1q, T.w1s, 1, T.w1t, W).then_inc(S.qw, 1)
-    v.wait_ge(S.zh1, 1)
-    act_v(T.ht, 0, 2, T.p1).then_inc(S.ah, 1)
-    act_v(T.ht, 0, 3, T.p1).then_inc(S.ah, 1)
-    v.wait_ge(S.ah, 4)
-    quant(T.nq, T.ns, h_i, T.ht, 0).then_inc(S.hq, 1)
-    v.wait_ge(S.lda, 16)
-    quant(T.aq, T.as_, 0, T.at, 0).then_inc(S.qa0, 1)
-    v.wait_ge(S.ldb1, 16)
-    quant(T.bq, T.bs, f1, T.bt, f1 * W).then_inc(S.qa0, 1)
-    quant(T.aq, T.as_, 1, T.at, W).then_inc(S.qa1, 1)
-    v.wait_ge(S.ldb2, 16)
-    quant(T.bq, T.bs, f2, T.bt, f2 * W).then_inc(S.qb2, 1)
-    v.wait_ge(S.z11, 1)
-    act_v(T.got, 0, 2, T.p3).then_inc(S.a1, 1)
-    act_v(T.got, 0, 3, T.p3).then_inc(S.a1, 1)
-    v.wait_ge(S.a1, 4)
-    quant(T.goq, T.gos, 0, T.got, 0).then_inc(S.g1q, 1)
-    v.wait_ge(S.z21, 1)
-    act_v(T.got, W, 2, T.p5).then_inc(S.a2, 1)
-    act_v(T.got, W, 3, T.p5).then_inc(S.a2, 1)
-    v.wait_ge(S.a2, 4)
-    quant(T.goq, T.gos, 1, T.got, W).then_inc(S.g2q, 1)
-    v.wait_ge(S.ldbn, 16)
-    quant(T.bq, T.bs, near[0], T.bt, near[0] * W, 2).then_inc(S.qbn, 1)
-    v.wait_ge(S.ldw2, 16)
-    quant(T.w2q, T.w2s, 0, T.w2t, 0).then_inc(S.qw2, 1)
-    v.wait_ge(S.zn1, 1)
-    act_v(T.gnt, 0, 2, T.p7, 2).then_inc(S.an, 1)
-    act_v(T.gnt, 0, 3, T.p7, 2).then_inc(S.an, 1)
-    v.wait_ge(S.an, 4)
-    quant(T.nq, T.ns, 1, T.gnt, 0, 2).then_inc(S.gnq, 1)
-    v.wait_ge(S.yf, 1)
-    v.tensor_copy(T.yt[:, col(far[0], NC, 2)], T.p1[:, 0:2 * NC]).then_inc(S.ycf, 1)
-    hw, hn = W // 2, NC // 2
-    v.wait_ge(S.d0, 1)
-    v.tensor_copy(T.zt[:, 0:hw:4], T.p2[:, 0:hn]).then_inc(S.za, 1)
-    v.wait_ge(S.d1, 1)
-    v.tensor_copy(T.zt[:, 1:hw:4], T.p3[:, 0:hn]).then_inc(S.za, 1)
-    v.tensor_copy(T.zt[:, hw:W:4], T.p2[:, hn:NC]).then_inc(S.zb, 1)
-    v.tensor_copy(T.zt[:, hw + 1:W:4], T.p3[:, hn:NC]).then_inc(S.zb, 1)
+
+    def v_inputs(i):
+        j = JOBS[i]
+        if j == "h":
+            v.wait_ge(S.ldx, 16)
+            quant(T.xq, T.xs, 0, T.xt, 0).then_inc(S.qx, 1)
+            v.wait_ge(S.ldw1, 16)
+            quant(T.w1q, T.w1s, 0, T.w1t, 0).then_inc(S.qw0, 1)
+            quant(T.w1q, T.w1s, 1, T.w1t, W).then_inc(S.qw1, 1)
+            return
+        v.wait_ge(S["ld" + j], 16)
+        quant(T.bq, T.bs, rank[j], T.bt, rank[j] * W).then_inc(S["q" + j], 1)
+        if i == 0:
+            v.wait_ge(S.lda, 16)
+            quant(T.aq, T.as_, 0, T.at, 0).then_inc(S.qa0, 1)
+            quant(T.aq, T.as_, 1, T.at, W).then_inc(S.qa1, 1)
+
+    v_inputs(0)
+    for i, j in enumerate(JOBS):
+        v.wait_ge(S["z1" + j], 1)
+        o, z, f = result(j, 3)
+        v.tensor_scalar(o, z, f, 0.0, AluOpType.mult, AluOpType.max).then_inc(S["v1" + j], 1)
+        if i + 1 < len(JOBS):
+            v_inputs(i + 1)
+        else:
+            v.wait_ge(S.ldw2, 16)
+            quant(T.w2q, T.w2s, 0, T.w2t, 0).then_inc(S.qw2, 1)
+        v.wait_ge(S["v1" + j], 1)
+        v.wait_ge(S["ac" + j], 3)
+        quant(T.mq, T.ms, SLOT[j], T.tl, SLOT[j] * W).then_inc(S["mq" + j], 1)
+    v.wait_ge(S.y1, 1)
+    v.tensor_copy(T.yt[:, col(f1)], P[0][:, 0:NC]).then_inc(S.yc1, 1)
+    for b in (0, 1):
+        v.wait_ge(S["d%d" % b], 1)
+        v.tensor_copy(T.zt[:, b:W:4], zb[b][:, 0:NC]).then_inc(S.za, 1)
 
     t = g.tensor
-    t.wait_ge(S.qx0, 2)
-    mm(T.p0, T.w1q, T.w1s, 0, T.xq, T.xs, 0).then_inc(S.zh0, 1)
-    t.wait_ge(S.qw, 1)
-    mm(T.p1, T.w1q, T.w1s, 1, T.xq, T.xs, 0).then_inc(S.zh1, 1)
-    t.wait_ge(S.qa0, 2)
-    mm(T.p2, T.aq, T.as_, 0, T.bq, T.bs, f1).then_inc(S.z10, 1)
-    t.wait_ge(S.qa1, 1)
-    mm(T.p3, T.aq, T.as_, 1, T.bq, T.bs, f1).then_inc(S.z11, 1)
-    t.wait_ge(S.qb2, 1)
-    mm(T.p4, T.aq, T.as_, 0, T.bq, T.bs, f2).then_inc(S.z20, 1)
-    mm(T.p5, T.aq, T.as_, 1, T.bq, T.bs, f2).then_inc(S.z21, 1)
-    t.wait_ge(S.qbn, 1)
-    mm(T.p6, T.aq, T.as_, 0, T.bq, T.bs, near[0], 2).then_inc(S.zn0, 1)
-    mm(T.p7, T.aq, T.as_, 1, T.bq, T.bs, near[0], 2).then_inc(S.zn1, 1)
-    t.wait_ge(S.hq, 1)
-    t.wait_ge(S.qw2, 1)
-    mm(T.p0, T.w2q, T.w2s, 0, T.nq, T.ns, h_i).then_inc(S.yo, 1)
+    for i, j in enumerate(JOBS):
+        if i >= 4:
+            t.wait_ge(S["mq" + JOBS[i - 4]], 1)
+        lq, ls, rq, rs, ri = (T.w1q, T.w1s, T.xq, T.xs, 0) if j == "h" else (T.aq, T.as_, T.bq, T.bs, rank[j])
+        t.wait_ge(S.qx if j == "h" else S["q" + j], 1)
+        t.wait_ge(S.qw0 if j == "h" else S.qa0, 1)
+        mm(bank[j][0], lq, ls, 0, rq, rs, ri).then_inc(S["z0" + j], 1)
+        t.wait_ge(S.qw1 if j == "h" else S.qa1, 1)
+        mm(bank[j][1], lq, ls, 1, rq, rs, ri).then_inc(S["z1" + j], 1)
+
+    def slice_of_z(q, s, i, first=False, last=False):
+        for b in (0, 2, 1, 3):
+            m = mm(zb[b], T.sq, T.ss, b, q, s, i, first, last)
+            if last:
+                m.then_inc(S["d%d" % b], 1)
+
     t.wait_ge(S.qs, 4)
-    t.wait_ge(S.g1q, 1)
-    t.wait_ge(S.g2q, 1)
-    t.wait_ge(S.gnq, 1)
-    banks = [T.p2, T.p3, T.p4, T.p5]
-    order = [0, 2, 1, 3]
-    for b in order:
-        mm(banks[b], T.sq, T.ss, b, T.nq, T.ns, 1 + own_i, 1, True, False)
-    t.wait_ge(S.hin, 32)
-    mm(T.p1, T.w2q, T.w2s, 0, T.hlq, T.hls, 0, 2).then_inc(S.yf, 1)
+    t.wait_ge(S["mq" + JOBS[1]], 1)
+    t.wait_ge(S["mq" + JOBS[2]], 1)
+    t.wait_ge(S.f2in, 16)
+    slice_of_z(T.lq, T.ls, LAND["f2"], first=True)
+    t.wait_ge(S.mqo, 1)
+    slice_of_z(T.mq, T.ms, SLOT["o"])
+    t.wait_ge(S.qw2, 1)
+    t.wait_ge(S["mq" + JOBS[3]], 1)
+    mm(P[6], T.w2q, T.w2s, 0, T.mq, T.ms, SLOT["h"]).then_inc(S.yo, 1)
+    t.wait_ge(S.h1in, 16)
+    mm(P[0], T.w2q, T.w2s, 0, T.lq, T.ls, LAND["h1"]).then_inc(S.y1, 1)
+    t.wait_ge(S.hpin, 16)
+    mm(P[7], T.w2q, T.w2s, 0, T.lq, T.ls, LAND["hp"]).then_inc(S.yp, 1)
     t.wait_ge(S.pin, 16)
-    mm(T.p6, T.w2q, T.w2s, 0, T.plq, T.pls, ph_i).then_inc(S.yp, 1)
-    for b in order:
-        mm(banks[b], T.sq, T.ss, b, T.plq, T.pls, pg_i, 1, False, False)
-    t.wait_ge(S.g1in, 16)
-    for b in order:
-        mm(banks[b], T.sq, T.ss, b, T.glq, T.gls, 0, 1, False, False)
-    t.wait_ge(S.g2in, 16)
-    for b in order:
-        mm(banks[b], T.sq, T.ss, b, T.glq, T.gls, 1, 1, False, True).then_inc(S["d%d" % b], 1)
+    slice_of_z(T.lq, T.ls, LAND["p"])
+    t.wait_ge(S.f1in, 16)
+    slice_of_z(T.lq, T.ls, LAND["f1"], last=True)
+    t.wait_ge(S.h2in, 16)
+    mm(P[1], T.w2q, T.w2s, 0, T.lq, T.ls, LAND["h2"]).then_inc(S.y2, 1)
 
     s = g.scalar
-    s.wait_ge(S.zh0, 1)
-    act_s(T.ht, 0, 0, T.p0).then_inc(S.ah, 1)
-    act_s(T.ht, 0, 1, T.p0).then_inc(S.ah, 1)
-    s.wait_ge(S.z10, 1)
-    act_s(T.got, 0, 0, T.p2).then_inc(S.a1, 1)
-    act_s(T.got, 0, 1, T.p2).then_inc(S.a1, 1)
-    s.wait_ge(S.z20, 1)
-    act_s(T.got, W, 0, T.p4).then_inc(S.a2, 1)
-    act_s(T.got, W, 1, T.p4).then_inc(S.a2, 1)
-    s.wait_ge(S.zn0, 1)
-    act_s(T.gnt, 0, 0, T.p6, 2).then_inc(S.an, 1)
-    act_s(T.gnt, 0, 1, T.p6, 2).then_inc(S.an, 1)
+    for j in JOBS:
+        s.wait_ge(S["z0" + j], 1)
+        for b in (0, 1, 2):
+            if b == 2:
+                s.wait_ge(S["v1" + j], 1)
+            o, z, f = result(j, b)
+            s.activation(o, z, AF.Relu, scale=f).then_inc(S["ac" + j], 1)
     s.wait_ge(S.yo, 1)
-    s.activation(T.yt[:, col(r)], T.p0[:, 0:NC], AF.Copy).then_inc(S.ycn, 1)
+    s.activation(T.yt[:, col(r)], P[6][:, 0:NC], AF.Copy).then_inc(S.ycn, 1)
     s.wait_ge(S.yp, 1)
-    s.activation(T.yt[:, col(p)], T.p6[:, 0:NC], AF.Copy).then_inc(S.ycn, 1)
-    s.wait_ge(S.d2, 1)
-    s.activation(T.zt[:, 2:hw:4], T.p4[:, 0:hn], AF.Copy).then_inc(S.za, 1)
-    s.wait_ge(S.d3, 1)
-    s.activation(T.zt[:, 3:hw:4], T.p5[:, 0:hn], AF.Copy).then_inc(S.za, 1)
-    s.activation(T.zt[:, hw + 2:W:4], T.p4[:, hn:NC], AF.Copy).then_inc(S.zb, 1)
-    s.activation(T.zt[:, hw + 3:W:4], T.p5[:, hn:NC], AF.Copy).then_inc(S.zb, 1)
-    s.wait_ge(S.zb, 4)
-    s.dma_start(T.z[:, hw:W], T.zt[:, hw:W]).then_inc(S.stb, 16)
-    s.wait_ge(S.stb, 16)
+    s.activation(T.yt[:, col(p)], P[7][:, 0:NC], AF.Copy).then_inc(S.ycn, 1)
+    for b in (2, 3):
+        s.wait_ge(S["d%d" % b], 1)
+        s.activation(T.zt[:, b:W:4], zb[b][:, 0:NC], AF.Copy).then_inc(S.za, 1)
+    s.wait_ge(S.y2, 1)
+    s.activation(T.yt[:, col(f2)], P[1][:, 0:NC], AF.Copy).then_inc(S.yc2, 1)
+    s.wait_ge(S.yc2, 1)
+    s.dma_start(T.y[:, col(f2)], T.yt[:, col(f2)]).then_inc(S.sty2, 16)
+    s.wait_ge(S.sty2, 16)
 
-    g.sync.wait_ge(S.ycf, 1)
-    g.sync.dma_start(T.y[:, col(far[0], NC, 2)], T.yt[:, col(far[0], NC, 2)]).then_inc(S.sty, 16)
-    g.sync.wait_ge(S.ycn, 2)
-    g.sync.dma_start(T.y[:, col(near[0], NC, 2)], T.yt[:, col(near[0], NC, 2)]).then_inc(S.sty, 16)
-    g.sync.wait_ge(S.za, 4)
-    g.sync.dma_start(T.z[:, 0:hw], T.zt[:, 0:hw]).then_inc(S.stz, 16)
-    g.sync.wait_ge(S.sty, 32)
-    g.sync.wait_ge(S.stz, 16)
+    y = g.sync
+    y.wait_ge(S.yc1, 1)
+    y.dma_start(T.y[:, col(f1)], T.yt[:, col(f1)]).then_inc(S.sty1, 16)
+    y.wait_ge(S.ycn, 2)
+    y.dma_start(T.y[:, col(near[0], NC, 2)], T.yt[:, col(near[0], NC, 2)]).then_inc(S.styn, 16)
+    y.wait_ge(S.za, 4)
+    y.dma_start(T.z[:, :], T.zt[:]).then_inc(S.stz, 16)
+    for k in ("sty1", "styn", "stz"):
+        y.wait_ge(S[k], 16)
 
     g.wait_ge(S.e0, 1)
     ev = T.et[:, 3:W + 3:4]
@@ -234,23 +201,29 @@ def rank_program(g, core, T, topo):
 
     off_mask = topo.mask(core, cores[f1])
     on_mask = topo.mask(core, cores[p]) & ~off_mask
-    slot = {c: far_of(c).index(r) for c in far}
-    g.wait_ge(S.hq, 1)
-    g.remote_dma_fused([RemoteDMATransfer(
-        dst_ids=[dst(c) for c in (f1, f2)], dma_engine_mask=off_mask, remote_sem=S.hin,
-        srcs=[T.nq[:, col(h_i)].bitcast(dt.uint8)],
-        dsts=[T.hlq[:, col(slot[c])].bitcast(dt.uint8) for c in (f1, f2)])], local_sem=S.sent)
-    g.remote_dma_fused([RemoteDMATransfer(
-        dst_ids=[dst(c) for c in (f1, f2)], dma_engine_mask=off_mask, remote_sem=S.hin,
-        srcs=[T.ns[:, col(h_i)]], dsts=[T.hls[:, col(slot[c])] for c in (f1, f2)])], local_sem=S.sent)
-    for i, c in enumerate((f1, f2)):
+
+    def views(i, made):
+        q, s_ = (T.mq, T.ms) if made else (T.lq, T.ls)
+        return [q[:, col(i)].bitcast(dt.uint8), s_[:, col(i)]]
+
+    def send(c, mask, sem, land, srcs):
         rid, pid = topo.addr(cores[c], core)
-        sem = S["g%din" % (i + 1)]
-        g.wait_ge(S["g%dq" % (i + 1)], 1)
-        g.remote_dma(T.glq[:, col(i)].bitcast(dt.uint8), T.goq[:, col(i)].bitcast(dt.uint8), sem, S.sent, pid, rid, off_mask)
-        g.remote_dma(T.gls[:, col(i)], T.gos[:, col(i)], sem, S.sent, pid, rid, off_mask)
-    rid, pid = topo.addr(cores[p], core)
-    g.wait_ge(S.gnq, 1)
-    g.remote_dma(T.plq[:].bitcast(dt.uint8), T.nq[:, pv].bitcast(dt.uint8), S.pin, S.sent, pid, rid, on_mask)
-    g.remote_dma(T.pls[:], T.ns[:, pv], S.pin, S.sent, pid, rid, on_mask)
-    g.wait_ge(S.sent, 8 * off_mask.bit_count())
+        for src, out in zip(srcs, views(land, False)):
+            g.remote_dma(out, src, sem, S.sent, pid, rid, mask)
+        return 2 * mask.bit_count()
+
+    g.wait_ge(S.mqf2, 1)
+    sent = send(f2, off_mask, S.f2in, LAND["f2"], views(SLOT["f2"], True))
+    g.wait_ge(S.mqh, 1)
+    for src, out1, outp in zip(views(SLOT["h"], True), views(LAND["h1"], False), views(LAND["hp"], False)):
+        g.remote_dma_fused([
+            RemoteDMATransfer(dst_ids=[dst(f1)], dma_engine_mask=off_mask, remote_sem=S.h1in, srcs=[src], dsts=[out1]),
+            RemoteDMATransfer(dst_ids=[dst(p)], dma_engine_mask=on_mask, remote_sem=S.hpin, srcs=[src], dsts=[outp])], local_sem=S.sent)
+        sent += off_mask.bit_count() + on_mask.bit_count()
+    g.wait_ge(S.mqf1, 1)
+    sent += send(f1, off_mask, S.f1in, LAND["f1"], views(SLOT["f1"], True))
+    g.wait_ge(S.mqp, 1)
+    sent += send(p, on_mask, S.pin, LAND["p"], views(SLOT["p"], True))
+    g.wait_ge(S.h1in, 16)
+    sent += send(p, on_mask, S.h2in, LAND["h2"], views(LAND["h1"], False))
+    g.wait_ge(S.sent, sent)

import numpy as np
from concourse.bass import DstId, RemoteDMATransfer
from concourse.mybir import dt, AluOpType, ActivationFunctionType as AF

NC = 128
W = 4 * NC
C = float(np.float32(0.023))
JOBS = ["f2", "f1", "h", "p", "o"]
SLOT = {j: i for i, j in enumerate(JOBS)}
LAND = {"f2": 0, "f1": 1, "p": 2, "hp": 3, "h1": 4, "h2": 5}

SCRATCH = {
    "xt": ("sbuf", [128, W], "bfloat16"),
    "w1t": ("sbuf", [128, 2 * W], "bfloat16"),
    "w2t": ("sbuf", [128, W], "bfloat16"),
    "at": ("sbuf", [128, 2 * W], "bfloat16"),
    "bt": ("sbuf", [128, 4 * W], "bfloat16"),
    "et": ("sbuf", [128, W + 4], "bfloat16"),
    "tl": ("sbuf", [128, 5 * W], "bfloat16"),
    "xq": ("sbuf", [128, NC], "float8_e4m3fn_x4"), "xs": ("sbuf", [128, NC], "uint8"),
    "w1q": ("sbuf", [128, 2 * NC], "float8_e4m3fn_x4"), "w1s": ("sbuf", [128, 2 * NC], "uint8"),
    "w2q": ("sbuf", [128, NC], "float8_e4m3fn_x4"), "w2s": ("sbuf", [128, NC], "uint8"),
    "aq": ("sbuf", [128, 2 * NC], "float8_e4m3fn_x4"), "as_": ("sbuf", [128, 2 * NC], "uint8"),
    "bq": ("sbuf", [128, 4 * NC], "float8_e4m3fn_x4"), "bs": ("sbuf", [128, 4 * NC], "uint8"),
    "sq": ("sbuf", [128, 4 * NC], "float8_e4m3fn_x4"), "ss": ("sbuf", [128, 4 * NC], "uint8"),
    "mq": ("sbuf", [128, 5 * NC], "float8_e4m3fn_x4"), "ms": ("sbuf", [128, 5 * NC], "uint8"),
    "lq": ("sbuf", [128, 6 * NC], "float8_e4m3fn_x4"), "ls": ("sbuf", [128, 6 * NC], "uint8"),
    "yt": ("sbuf", [128, 4 * NC], "float32"),
    "zt": ("sbuf", [128, W], "float32"),
}
for k in range(8):
    SCRATCH["p%d" % k] = ("psum", [128, 512], "float32")
SEMAPHORES = ["ldx", "ldw1", "lda", "ldw2", "e0", "e1", "qs", "qx", "qw0", "qw1", "qa0", "qa1", "qw2",
              "yo", "yp", "y1", "y2", "yc1", "yc2", "ycn", "d0", "d1", "d2", "d3", "za",
              "h1in", "h2in", "hpin", "f1in", "f2in", "pin", "sent", "styn", "sty1", "sty2", "stz"]
for j in JOBS:
    SEMAPHORES += ["ld" + j, "q" + j, "z0" + j, "z1" + j, "v1" + j, "ac" + j, "mq" + j]


def rank_program(g, core, T, topo):
    r = T.rank_of(core)
    if r is None:
        return
    cores = T.cores
    n = len(cores)
    S = T.sem

    near = [c for c in range(n) if topo.host(cores[c]) == topo.host(core) and topo.chip(cores[c]) == topo.chip(core)]
    far = [c for c in range(n) if c not in near]
    p = [c for c in near if c != r][0]
    f1 = [c for c in far if topo.die(cores[c]) == topo.die(core)][0]
    f2 = [c for c in far if c != f1][0]
    rank = {"f1": f1, "f2": f2, "p": p, "o": r}
    P = [T["p%d" % k] for k in range(8)]
    bank = {j: (P[2 * i % 8], P[2 * i % 8 + 1]) for i, j in enumerate(JOBS)}
    zb = P[2:6]

    def col(i, w=NC, k=1):
        return slice(i * w, (i + k) * w)

    def dst(c):
        rid, pid = topo.addr(cores[c], core)
        return DstId(rid=rid, pnc=pid)

    def quant(q, s, qi, src, lo):
        return g.vector.quantize_mx(q[:, col(qi)], s[:, col(qi)], src[:, lo:lo + W])

    def mm(out, lq, ls, li, rq, rs, ri, start=True, stop=True):
        return g.tensor.matmul_mx(out[:, 0:NC], lq[:, col(li)], ls[:, col(li)], rq[:, col(ri)], rs[:, col(ri)], start, stop)

    def result(j, b):
        lo = SLOT[j] * W
        return T.tl[:, lo + b:lo + W:4], bank[j][b // 2][:, 0:NC], C if b % 2 == 0 else -C

    def load_b(q, j):
        c = col(rank[j], W)
        q.dma_start(T.bt[:, c], T.b[:, c]).then_inc(S["ld" + j], 16)

    g.sync.dma_start(T.at[:], T.a[:, :]).then_inc(S.lda, 16)
    load_b(g.scalar, "f2")
    g.sync.dma_start(T.xt[:], T.x[:, :]).then_inc(S.ldx, 16)
    load_b(g.scalar, "f1")
    load_b(g.sync, "p")
    g.scalar.dma_start(T.w1t[:], T.w1[:, :]).then_inc(S.ldw1, 16)
    g.sync.dma_start(T.w2t[:], T.w2[:, :]).then_inc(S.ldw2, 16)
    load_b(g.scalar, "o")

    v = g.vector
    v.memset(T.et[:], 0.0).then_inc(S.e0, 1)
    v.wait_ge(S.e1, 1)
    for b in range(4):
        quant(T.sq, T.ss, b, T.et, 3 - b).then_inc(S.qs, 1)

    def v_inputs(i):
        j = JOBS[i]
        if j == "h":
            v.wait_ge(S.ldx, 16)
            quant(T.xq, T.xs, 0, T.xt, 0).then_inc(S.qx, 1)
            v.wait_ge(S.ldw1, 16)
            quant(T.w1q, T.w1s, 0, T.w1t, 0).then_inc(S.qw0, 1)
            quant(T.w1q, T.w1s, 1, T.w1t, W).then_inc(S.qw1, 1)
            return
        v.wait_ge(S["ld" + j], 16)
        quant(T.bq, T.bs, rank[j], T.bt, rank[j] * W).then_inc(S["q" + j], 1)
        if i == 0:
            v.wait_ge(S.lda, 16)
            quant(T.aq, T.as_, 0, T.at, 0).then_inc(S.qa0, 1)
            quant(T.aq, T.as_, 1, T.at, W).then_inc(S.qa1, 1)

    v_inputs(0)
    for i, j in enumerate(JOBS):
        v.wait_ge(S["z1" + j], 1)
        o, z, f = result(j, 3)
        v.tensor_scalar(o, z, f, 0.0, AluOpType.mult, AluOpType.max).then_inc(S["v1" + j], 1)
        if i + 1 < len(JOBS):
            v_inputs(i + 1)
        else:
            v.wait_ge(S.ldw2, 16)
            quant(T.w2q, T.w2s, 0, T.w2t, 0).then_inc(S.qw2, 1)
        v.wait_ge(S["v1" + j], 1)
        v.wait_ge(S["ac" + j], 3)
        quant(T.mq, T.ms, SLOT[j], T.tl, SLOT[j] * W).then_inc(S["mq" + j], 1)
    v.wait_ge(S.y1, 1)
    v.tensor_copy(T.yt[:, col(f1)], P[0][:, 0:NC]).then_inc(S.yc1, 1)
    for b in (0, 1):
        v.wait_ge(S["d%d" % b], 1)
        v.tensor_copy(T.zt[:, b:W:4], zb[b][:, 0:NC]).then_inc(S.za, 1)

    t = g.tensor
    for i, j in enumerate(JOBS):
        if i >= 4:
            t.wait_ge(S["mq" + JOBS[i - 4]], 1)
        lq, ls, rq, rs, ri = (T.w1q, T.w1s, T.xq, T.xs, 0) if j == "h" else (T.aq, T.as_, T.bq, T.bs, rank[j])
        t.wait_ge(S.qx if j == "h" else S["q" + j], 1)
        t.wait_ge(S.qw0 if j == "h" else S.qa0, 1)
        mm(bank[j][0], lq, ls, 0, rq, rs, ri).then_inc(S["z0" + j], 1)
        t.wait_ge(S.qw1 if j == "h" else S.qa1, 1)
        mm(bank[j][1], lq, ls, 1, rq, rs, ri).then_inc(S["z1" + j], 1)

    def slice_of_z(q, s, i, first=False, last=False):
        for b in (0, 2, 1, 3):
            m = mm(zb[b], T.sq, T.ss, b, q, s, i, first, last)
            if last:
                m.then_inc(S["d%d" % b], 1)

    t.wait_ge(S.qs, 4)
    t.wait_ge(S["mq" + JOBS[1]], 1)
    t.wait_ge(S["mq" + JOBS[2]], 1)
    t.wait_ge(S.f2in, 16)
    slice_of_z(T.lq, T.ls, LAND["f2"], first=True)
    t.wait_ge(S.mqo, 1)
    slice_of_z(T.mq, T.ms, SLOT["o"])
    t.wait_ge(S.qw2, 1)
    t.wait_ge(S["mq" + JOBS[3]], 1)
    mm(P[6], T.w2q, T.w2s, 0, T.mq, T.ms, SLOT["h"]).then_inc(S.yo, 1)
    t.wait_ge(S.h1in, 16)
    mm(P[0], T.w2q, T.w2s, 0, T.lq, T.ls, LAND["h1"]).then_inc(S.y1, 1)
    t.wait_ge(S.hpin, 16)
    mm(P[7], T.w2q, T.w2s, 0, T.lq, T.ls, LAND["hp"]).then_inc(S.yp, 1)
    t.wait_ge(S.pin, 16)
    slice_of_z(T.lq, T.ls, LAND["p"])
    t.wait_ge(S.f1in, 16)
    slice_of_z(T.lq, T.ls, LAND["f1"], last=True)
    t.wait_ge(S.h2in, 16)
    mm(P[1], T.w2q, T.w2s, 0, T.lq, T.ls, LAND["h2"]).then_inc(S.y2, 1)

    s = g.scalar
    for j in JOBS:
        s.wait_ge(S["z0" + j], 1)
        for b in (0, 1, 2):
            if b == 2:
                s.wait_ge(S["v1" + j], 1)
            o, z, f = result(j, b)
            s.activation(o, z, AF.Relu, scale=f).then_inc(S["ac" + j], 1)
    s.wait_ge(S.yo, 1)
    s.activation(T.yt[:, col(r)], P[6][:, 0:NC], AF.Copy).then_inc(S.ycn, 1)
    s.wait_ge(S.yp, 1)
    s.activation(T.yt[:, col(p)], P[7][:, 0:NC], AF.Copy).then_inc(S.ycn, 1)
    for b in (2, 3):
        s.wait_ge(S["d%d" % b], 1)
        s.activation(T.zt[:, b:W:4], zb[b][:, 0:NC], AF.Copy).then_inc(S.za, 1)
    s.wait_ge(S.y2, 1)
    s.activation(T.yt[:, col(f2)], P[1][:, 0:NC], AF.Copy).then_inc(S.yc2, 1)
    s.wait_ge(S.yc2, 1)
    s.dma_start(T.y[:, col(f2)], T.yt[:, col(f2)]).then_inc(S.sty2, 16)
    s.wait_ge(S.sty2, 16)

    y = g.sync
    y.wait_ge(S.yc1, 1)
    y.dma_start(T.y[:, col(f1)], T.yt[:, col(f1)]).then_inc(S.sty1, 16)
    y.wait_ge(S.ycn, 2)
    y.dma_start(T.y[:, col(near[0], NC, 2)], T.yt[:, col(near[0], NC, 2)]).then_inc(S.styn, 16)
    y.wait_ge(S.za, 4)
    y.dma_start(T.z[:, :], T.zt[:]).then_inc(S.stz, 16)
    for k in ("sty1", "styn", "stz"):
        y.wait_ge(S[k], 16)

    g.wait_ge(S.e0, 1)
    ev = T.et[:, 3:W + 3:4]
    g.affine_select(ev, ev, [[-1, NC]], AluOpType.not_equal, 1.0, 0, 1).then_inc(S.e1, 1)

    off_mask = topo.mask(core, cores[f1])
    on_mask = topo.mask(core, cores[p]) & ~off_mask

    def views(i, made):
        q, s_ = (T.mq, T.ms) if made else (T.lq, T.ls)
        return [q[:, col(i)].bitcast(dt.uint8), s_[:, col(i)]]

    def send(c, mask, sem, land, srcs):
        rid, pid = topo.addr(cores[c], core)
        for src, out in zip(srcs, views(land, False)):
            g.remote_dma(out, src, sem, S.sent, pid, rid, mask)
        return 2 * mask.bit_count()

    g.wait_ge(S.mqf2, 1)
    sent = send(f2, off_mask, S.f2in, LAND["f2"], views(SLOT["f2"], True))
    g.wait_ge(S.mqh, 1)
    for src, out1, outp in zip(views(SLOT["h"], True), views(LAND["h1"], False), views(LAND["hp"], False)):
        g.remote_dma_fused([
            RemoteDMATransfer(dst_ids=[dst(f1)], dma_engine_mask=off_mask, remote_sem=S.h1in, srcs=[src], dsts=[out1]),
            RemoteDMATransfer(dst_ids=[dst(p)], dma_engine_mask=on_mask, remote_sem=S.hpin, srcs=[src], dsts=[outp])], local_sem=S.sent)
        sent += off_mask.bit_count() + on_mask.bit_count()
    g.wait_ge(S.mqf1, 1)
    sent += send(f1, off_mask, S.f1in, LAND["f1"], views(SLOT["f1"], True))
    g.wait_ge(S.mqp, 1)
    sent += send(p, on_mask, S.pin, LAND["p"], views(SLOT["p"], True))
    g.wait_ge(S.h1in, 16)
    sent += send(p, on_mask, S.h2in, LAND["h2"], views(LAND["h1"], False))
    g.wait_ge(S.sent, sent)
